import numpy as np
import ml_dtypes


def mxq(x, axis, fmt="e4m3"):
    dtype, down = {"e4m3": (ml_dtypes.float8_e4m3fn, 7), "e5m2": (ml_dtypes.float8_e5m2, 14)}[fmt]
    v = np.moveaxis(np.asarray(x, np.float32).astype(ml_dtypes.bfloat16).astype(np.float64), axis, -1)
    blocks = v.reshape(v.shape[:-1] + (-1, 32))
    amax = np.abs(blocks).max(-1, keepdims=True)
    byte = np.maximum(np.where(amax > 0, np.frexp(amax)[1] - 1 + 127, 0) - down, 1)
    scale = np.exp2(byte - 127.0)
    codes = (blocks / scale).astype(np.float32).astype(dtype).astype(np.float64)
    return np.moveaxis((codes * scale).reshape(v.shape), -1, axis)


WIDE = False


def mx_kscale(k):
    if not WIDE:
        return np.ones(k)
    levels = np.array([10, -10, 5, -5, 0])
    if k % 512:
        return np.exp2(np.random.permutation(np.resize(levels, k // 32))).repeat(32)
    a = np.empty((k // 512, 16))
    for p in range(k // 512):
        a[p, :8] = np.random.permutation(np.resize(levels, 8))
        for g in range(8):
            far = levels[np.abs(levels - a[p, g]) >= 10]
            a[p, g + 8] = far[np.random.randint(len(far))]
    return np.exp2(a.ravel()).repeat(32)


def f64(x):
    return np.asarray(x).astype(np.float64)


def striped(idx):
    return np.tile(idx.reshape(-1, 16).T, (8, 1)).astype(np.uint16)


def unstriped(offs):
    return offs[:16].T.reshape(-1).astype(np.int64)


def pack_weight(w):
    k, n = w.shape
    w = f64(np.asarray(w, np.float32).astype(ml_dtypes.bfloat16)).reshape(k // 32, 32, n)
    amax = np.abs(w).max(1)
    byte = np.clip(np.where(amax > 0, np.frexp(amax)[1] - 1 + 127 - 7, 1), 1, 254)
    scaled = (w * np.exp2(127.0 - byte)[:, None, :]).reshape(k, n).astype(np.float32)
    words = np.ascontiguousarray(scaled.reshape(k // 512, 128, 4, n).transpose(0, 1, 3, 2)).astype(ml_dtypes.float8_e4m3fn).view(np.uint8)
    return words, np.ascontiguousarray(byte.astype(np.uint8).reshape(k // 512, 16, n))


def unpack_weight(words, scales):
    g, p, n, _ = words.shape
    vals = np.ascontiguousarray(words).view(ml_dtypes.float8_e4m3fn).astype(np.float64) * np.repeat(np.exp2(scales.astype(np.float64) - 127.0), 8, axis=1)[..., None]
    return vals.transpose(0, 1, 3, 2).reshape(g * 512, n)


E2M1 = np.array([0.0, 0.5, 1.0, 1.5, 2.0, 3.0, 4.0, 6.0, -0.0, -0.5, -1.0, -1.5, -2.0, -3.0, -4.0, -6.0])


def pack_fp4(w):
    k, n = w.shape
    w = f64(np.asarray(w, np.float32).astype(ml_dtypes.bfloat16)).reshape(k // 32, 32, n)
    amax = np.abs(w).max(1)
    mant, ex = np.frexp(amax / 6.0)
    byte = np.clip(np.where(amax > 0, np.where(mant > 0.5, ex, ex - 1) + 127, 1), 1, 254)
    scaled = (w * np.exp2(127.0 - byte)[:, None, :]).reshape(k, n).astype(np.float32)
    c = np.ascontiguousarray(scaled.reshape(k // 512, 128, 4, n).transpose(0, 1, 3, 2)).astype(ml_dtypes.float4_e2m1fn).view(np.uint8) & 0xF
    words = (c[..., 0::2] | (c[..., 1::2] << 4)).reshape(k // 512, 128, 2 * n)
    return np.ascontiguousarray(words), np.ascontiguousarray(byte.astype(np.uint8).reshape(k // 512, 16, n))


def unpack_fp4(words, scales):
    g, _, n = scales.shape
    words = np.ascontiguousarray(words).reshape(g, 128, n, 2)
    nib = np.empty((g, 128, n, 4), np.uint8)
    nib[..., 0::2] = words & 0xF
    nib[..., 1::2] = words >> 4
    vals = E2M1[nib] * np.repeat(np.exp2(scales.astype(np.float64) - 127.0), 8, axis=1)[..., None]
    return vals.transpose(0, 1, 3, 2).reshape(g * 512, n)


def relu(v):
    return np.maximum(v, 0.0)


K, T, S, V, H, N = 1024, 1024, 512, 256, 512, 128


def setup_inputs():
    n = np.random.standard_normal
    s = mx_kscale(K)[:, None]
    u = mx_kscale(H)
    packed_xT = pack_weight(n((K, T)) * s)
    packed_w2 = pack_fp4(n((H, N)) / np.sqrt(H) / u[:, None])
    return {
        "x_words": packed_xT[0],
        "x_scales": packed_xT[1],
        "w1": (n((K, H)) / np.sqrt(K) / s * u).astype(np.float32),
        "w2_words": packed_w2[0],
        "w2_scales": packed_w2[1],
        "offs": striped(np.random.permutation(T)[:S]),
    }


def reference(x_words, x_scales, w1, w2_words, w2_scales, offs):
    xq = unpack_weight(x_words, x_scales)[:, unstriped(offs)]
    h = relu(mxq(f64(w1), 0, "e4m3").T @ xq)
    z = np.abs(h[:, :V] - h[:, V:2 * V])
    return unpack_fp4(w2_words, w2_scales).T @ mxq(z, 0, "e4m3")

@@ -1,0 +1,174 @@
+from contextlib import ExitStack
+
+import concourse.mybir as mybir
+
+K, T, S, V, H, N = 1024, 1024, 512, 256, 512, 128
+FLOPS = 2 * K * H * S + 2 * H * N * V
+
+F32 = mybir.dt.float32
+BF16 = mybir.dt.bfloat16
+I32 = mybir.dt.int32
+U32 = mybir.dt.uint32
+U16 = mybir.dt.uint16
+U8 = mybir.dt.uint8
+FP8X4 = mybir.dt.float8_e4m3fn_x4
+FP4X4 = mybir.dt.float4_e2m1fn_x4
+ACT = mybir.ActivationFunctionType
+ALU = mybir.AluOpType
+
+P = 128
+PACK = 4
+K_PASS = P * PACK
+PASSES = K // K_PASS
+HALF_M = P // 2
+HALF_V = V // 2
+
+W1_LOADS = [(0, 0, 64), (0, 64, 128), (1, 0, 64), (1, 64, 96), (1, 96, 128)]
+W1_CASTS = [(0, 0, 64, "s"), (1, 64, 100, "v"), (1, 100, 128, "s"), (2, 0, 24, "v"), (2, 24, 64, "s"), (3, 64, 96, "s"), (4, 96, 118, "v"), (4, 118, 128, "s")]
+
+
+def tile_picked_siam_abs_p_kernel(tc, x_words, x_scales, w1, w2_words, w2_scales, offs, out):
+    nc = tc.nc
+    with ExitStack() as ctx:
+        keep = ctx.enter_context(tc.tile_pool(name="keep", bufs=1))
+        psum = ctx.enter_context(tc.psum_pool(name="psum", bufs=1))
+
+        offsets = keep.tile([P, S // 16], U16, name="offsets")
+        x_scale_table = keep.tile([P, T], U8, name="x_scale_table", align_bytes=64)
+        w2_scale = keep.tile([P, N], U8, name="w2_scale", align_bytes=64)
+        w2_codes = keep.tile([P, 2 * N], U8, name="w2_codes", align_bytes=64)
+        x_table = [keep.tile([P, T], U32, name=f"x_table{z}", align_bytes=64) for z in range(PASSES)]
+        w1_raw = [keep.tile([P, PACK, PACK * (m1 - m0)], F32, name=f"w1_raw{c}", align_bytes=64) for c, (z, m0, m1) in enumerate(W1_LOADS)]
+
+        nc.vector.memset(x_scale_table[:].bitcast(I32), 0)
+        nc.gpsimd.memset(w2_scale[:].bitcast(I32), 0)
+
+        def load_w1(c):
+            z, m0, m1 = W1_LOADS[c]
+            rows = w1[z * K_PASS : (z + 1) * K_PASS, PACK * m0 : PACK * m1]
+            nc.sync.dma_start(out=w1_raw[c][:], in_=rows.rearrange("(p j) c -> p j c", j=PACK))
+
+        def load_x(z):
+            nc.sync.dma_start(out=x_table[z][:].bitcast(I32), in_=x_words[z].rearrange("p c r -> p (c r)").bitcast(I32))
+
+        for q in range(4):
+            nc.scalar.dma_start(
+                out=x_scale_table[32 * q : 32 * q + 4 * PASSES, :].bitcast(I32),
+                in_=x_scales[:, 4 * q : 4 * q + 4, :].bitcast(I32),
+            )
+        load_x(0)
+        nc.sync.dma_start(offsets[:], offs)
+        load_w1(0)
+        load_w1(1)
+        load_x(1)
+        load_w1(2)
+        load_w1(3)
+        load_w1(4)
+        nc.sync.dma_start(out=w2_codes[:].bitcast(I32), in_=w2_words[0].bitcast(I32))
+        for q in range(4):
+            nc.sync.dma_start(
+                out=w2_scale[32 * q : 32 * q + 4, :].bitcast(I32),
+                in_=w2_scales[0, 4 * q : 4 * q + 4, :].bitcast(I32),
+            )
+
+        w1_bf = [keep.tile([P, PACK, P, PACK], BF16, name=f"w1_bf{z}", align_bytes=64) for z in range(PASSES)]
+        w1_codes = [keep.tile([P, PACK, P], U32, name=f"w1_codes{z}", align_bytes=64) for z in range(PASSES)]
+        w1_scale = [keep.tile([P, PACK, P], U8, name=f"w1_scale{z}", align_bytes=64) for z in range(PASSES)]
+
+        def cast_w1(c, m0, m1, engine):
+            z, first, last = W1_LOADS[c]
+            dst = w1_bf[z][:, :, m0:m1, :].rearrange("p t m j -> p m j t")
+            src = w1_raw[c][:, :, PACK * (m0 - first) : PACK * (m1 - first)].rearrange("p j (m t) -> p m j t", t=PACK)
+            if engine == "v":
+                nc.vector.tensor_copy(out=dst, in_=src)
+            else:
+                nc.scalar.activation(out=dst, in_=src, func=ACT.Copy)
+
+        def quantize_w1(z, t0, t1, m0, m1):
+            nc.vector.quantize_mx(
+                out=w1_codes[z][:, t0:t1, m0:m1].rearrange("p t m -> p (t m)").bitcast(FP8X4),
+                scales=w1_scale[z][:, t0:t1, m0:m1].rearrange("p t m -> p (t m)"),
+                in_=w1_bf[z][:, t0:t1, m0:m1, :].rearrange("p t m j -> p (t m j)"),
+            )
+
+        x_scale = keep.tile([P, S], U8, name="x_scale", align_bytes=64)
+        x_codes = [keep.tile([P, S], U32, name=f"x_codes{z}", align_bytes=64) for z in range(PASSES)]
+        acc = [[psum.tile([P, V], F32, name=f"acc{t}_{side}", tag=f"bank{t}_{side}") for side in range(2)] for t in range(PACK)]
+
+        def layer1(z, t, side):
+            cols = slice(side * V, (side + 1) * V)
+            nc.tensor.matmul_mx(
+                out=acc[t][side][:],
+                lhsT=w1_codes[z][:, t, :].bitcast(FP8X4),
+                lhsT_scale=w1_scale[z][:, t, :],
+                rhs=x_codes[z][:, cols].bitcast(FP8X4),
+                rhs_scale=x_scale[4 * z :, cols],
+                start=(z == 0),
+                stop=(z == PASSES - 1),
+            )
+
+        cast_w1(*W1_CASTS[0])
+        nc.vector.tensor_copy(x_codes[0][:], x_table[0][:].indirect(offsets[:]))
+        nc.vector.tensor_copy(x_scale[:], x_scale_table[:].indirect(offsets[:]))
+        cast_w1(*W1_CASTS[1])
+        cast_w1(*W1_CASTS[2])
+        for t in range(PACK):
+            if t % 2 == 0:
+                quantize_w1(0, t, t + 2, 0, P)
+            layer1(0, t, 1)
+            layer1(0, t, 0)
+        nc.vector.tensor_copy(x_codes[1][:], x_table[1][:].indirect(offsets[:]))
+        cast_w1(*W1_CASTS[3])
+        cast_w1(*W1_CASTS[4])
+        for t in range(PACK):
+            quantize_w1(1, t, t + 1, 0, HALF_M)
+        for cast in W1_CASTS[5:]:
+            cast_w1(*cast)
+
+        second = keep.tile([P, PACK, V], F32, name="second")
+        diff = keep.tile([P, PACK, V], F32, name="diff")
+        for t in range(PACK):
+            quantize_w1(1, t, t + 1, HALF_M, P)
+            layer1(1, t, 1)
+            layer1(1, t, 0)
+        for t in range(PACK):
+            nc.scalar.activation(out=second[:, t, :], in_=acc[t][1][:], func=ACT.Relu)
+            for cols in ([slice(0, V)] if t < PACK - 1 else [slice(0, HALF_V), slice(HALF_V, V)]):
+                nc.vector.scalar_tensor_tensor(
+                    out=diff[:, t, cols], in0=acc[t][0][:, cols], scalar=0.0, in1=second[:, t, cols], op0=ALU.max, op1=ALU.subtract
+                )
+
+        z_bf = [keep.tile([P, HALF_V, PACK], BF16, name=f"z_bf{h}", align_bytes=64) for h in range(2)]
+        z_codes = [keep.tile([P, HALF_V], U32, name=f"z_codes{h}", align_bytes=64) for h in range(2)]
+        z_scale = [keep.tile([P, HALF_V], U8, name=f"z_scale{h}", align_bytes=64) for h in range(2)]
+        nc.scalar.activation(
+            out=z_bf[1][:].rearrange("p (c i) t -> p c t i", i=4),
+            in_=diff[:, :, HALF_V:].rearrange("p t (c i) -> p c t i", i=4),
+            func=ACT.Abs,
+        )
+        first_half = diff[:, :, :HALF_V].rearrange("p t v -> p v t")
+        nc.vector.scalar_tensor_tensor(out=z_bf[0][:], in0=first_half, scalar=-1.0, in1=first_half, op0=ALU.mult, op1=ALU.max)
+
+        for h in range(2):
+            nc.vector.quantize_mx(
+                out=z_codes[h][:].bitcast(FP8X4), scales=z_scale[h][:], in_=z_bf[h][:].rearrange("p v t -> p (v t)")
+            )
+        for h in range(2):
+            res = psum.tile([N, V], F32, name=f"res{h}", tag=f"bank{h}_1")
+            nc.tensor.matmul_mx(
+                out=res[:, :HALF_V],
+                lhsT=w2_codes[:].bitcast(FP4X4),
+                lhsT_scale=w2_scale[:],
+                rhs=z_codes[h][:].bitcast(FP8X4),
+                rhs_scale=z_scale[h][:],
+                start=True,
+                stop=True,
+            )
+            staged = keep.tile([N, HALF_V], F32, name=f"staged{h}")
+            cols = slice(h * HALF_V, (h + 1) * HALF_V)
+            if h == 0:
+                nc.scalar.copy(out=staged[:], in_=res[:, :HALF_V])
+                nc.scalar.dma_start(out=out[:, cols], in_=staged[:])
+            else:
+                nc.vector.tensor_copy(out=staged[:], in_=res[:, :HALF_V])
+                nc.sync.dma_start(out=out[:, cols], in_=staged[:])

@@ -23,8 +23,8 @@ PASSES = K // K_PASS
 HALF_M = P // 2
 HALF_V = V // 2
 
-W1_LOADS = [(0, 0, 64), (0, 64, 128), (1, 0, 64), (1, 64, 96), (1, 96, 128)]
-W1_CASTS = [(0, 0, 64, "s"), (1, 64, 100, "v"), (1, 100, 128, "s"), (2, 0, 24, "v"), (2, 24, 64, "s"), (3, 64, 96, "s"), (4, 96, 118, "v"), (4, 118, 128, "s")]
+W1_LOADS = [(0, 0, 128), (1, 0, 64), (1, 64, 128)]
+W1_CASTS = [(0, 0, 84, "v"), (0, 84, 128, "s"), (1, 0, 16, "v"), (1, 16, 64, "s"), (2, 64, 106, "v"), (2, 106, 128, "s")]
 
 
 def tile_picked_siam_abs_p_kernel(tc, x_words, x_scales, w1, w2_words, w2_scales, offs, out):
@@ -38,13 +38,14 @@ def tile_picked_siam_abs_p_kernel(tc, x_words, x_scales, w1, w2_words, w2_scales
         w2_scale = keep.tile([P, N], U8, name="w2_scale", align_bytes=64)
         w2_codes = keep.tile([P, 2 * N], U8, name="w2_codes", align_bytes=64)
         x_table = [keep.tile([P, T], U32, name=f"x_table{z}", align_bytes=64) for z in range(PASSES)]
-        w1_raw = [keep.tile([P, PACK, PACK * (m1 - m0)], F32, name=f"w1_raw{c}", align_bytes=64) for c, (z, m0, m1) in enumerate(W1_LOADS)]
+        w1_raw = {}
 
         nc.vector.memset(x_scale_table[:].bitcast(I32), 0)
-        nc.gpsimd.memset(w2_scale[:].bitcast(I32), 0)
+        nc.vector.memset(w2_scale[:].bitcast(I32), 0)
 
         def load_w1(c):
             z, m0, m1 = W1_LOADS[c]
+            w1_raw[c] = keep.tile([P, PACK, PACK * (m1 - m0)], F32, name=f"w1_raw{c}", tag=f"w1_raw{c}", align_bytes=64)
             rows = w1[z * K_PASS : (z + 1) * K_PASS, PACK * m0 : PACK * m1]
             nc.sync.dma_start(out=w1_raw[c][:], in_=rows.rearrange("(p j) c -> p j c", j=PACK))
 
@@ -56,14 +57,12 @@ def tile_picked_siam_abs_p_kernel(tc, x_words, x_scales, w1, w2_words, w2_scales
                 out=x_scale_table[32 * q : 32 * q + 4 * PASSES, :].bitcast(I32),
                 in_=x_scales[:, 4 * q : 4 * q + 4, :].bitcast(I32),
             )
-        load_x(0)
         nc.sync.dma_start(offsets[:], offs)
+        load_x(0)
         load_w1(0)
-        load_w1(1)
         load_x(1)
+        load_w1(1)
         load_w1(2)
-        load_w1(3)
-        load_w1(4)
         nc.sync.dma_start(out=w2_codes[:].bitcast(I32), in_=w2_words[0].bitcast(I32))
         for q in range(4):
             nc.sync.dma_start(
@@ -71,92 +70,98 @@ def tile_picked_siam_abs_p_kernel(tc, x_words, x_scales, w1, w2_words, w2_scales
                 in_=w2_scales[0, 4 * q : 4 * q + 4, :].bitcast(I32),
             )
 
-        w1_bf = [keep.tile([P, PACK, P, PACK], BF16, name=f"w1_bf{z}", align_bytes=64) for z in range(PASSES)]
         w1_codes = [keep.tile([P, PACK, P], U32, name=f"w1_codes{z}", align_bytes=64) for z in range(PASSES)]
         w1_scale = [keep.tile([P, PACK, P], U8, name=f"w1_scale{z}", align_bytes=64) for z in range(PASSES)]
 
-        def cast_w1(c, m0, m1, engine):
+        def cast_w1(rounded, rounded_first, c, m0, m1, engine):
             z, first, last = W1_LOADS[c]
-            dst = w1_bf[z][:, :, m0:m1, :].rearrange("p t m j -> p m j t")
+            dst = rounded[:, :, m0 - rounded_first : m1 - rounded_first, :].rearrange("p t m j -> p m j t")
             src = w1_raw[c][:, :, PACK * (m0 - first) : PACK * (m1 - first)].rearrange("p j (m t) -> p m j t", t=PACK)
             if engine == "v":
                 nc.vector.tensor_copy(out=dst, in_=src)
             else:
                 nc.scalar.activation(out=dst, in_=src, func=ACT.Copy)
 
-        def quantize_w1(z, t0, t1, m0, m1):
+        def quantize_w1(rounded, z, t0, t1, m0, m1):
             nc.vector.quantize_mx(
                 out=w1_codes[z][:, t0:t1, m0:m1].rearrange("p t m -> p (t m)").bitcast(FP8X4),
                 scales=w1_scale[z][:, t0:t1, m0:m1].rearrange("p t m -> p (t m)"),
-                in_=w1_bf[z][:, t0:t1, m0:m1, :].rearrange("p t m j -> p (t m j)"),
+                in_=rounded[:, t0:t1, :, :].rearrange("p t m j -> p (t m j)"),
             )
 
-        x_scale = keep.tile([P, S], U8, name="x_scale", align_bytes=64)
-        x_codes = [keep.tile([P, S], U32, name=f"x_codes{z}", align_bytes=64) for z in range(PASSES)]
-        acc = [[psum.tile([P, V], F32, name=f"acc{t}_{side}", tag=f"bank{t}_{side}") for side in range(2)] for t in range(PACK)]
+        x_scale = keep.tile([P, 2, 2, HALF_V], U8, name="x_scale", align_bytes=64)
+        x_codes = {0: keep.tile([P, 2, 2, HALF_V], U32, name="x_codes0", align_bytes=64)}
+        acc = [[psum.tile([P, 2, HALF_V], F32, name=f"acc{h}_{t}", tag=f"bank{h}_{t}") for t in range(PACK)] for h in range(2)]
 
-        def layer1(z, t, side):
-            cols = slice(side * V, (side + 1) * V)
+        def gather_pieces(picked, table):
+            for h in range(2):
+                for side in range(2):
+                    first = (side * V + h * HALF_V) // 16
+                    nc.vector.tensor_copy(picked[:, h, side, :], table[:].indirect(offsets[:, first : first + HALF_V // 16]))
+
+        def layer1(z, t, h):
             nc.tensor.matmul_mx(
-                out=acc[t][side][:],
+                out=acc[h][t][:].rearrange("p s v -> p (s v)"),
                 lhsT=w1_codes[z][:, t, :].bitcast(FP8X4),
                 lhsT_scale=w1_scale[z][:, t, :],
-                rhs=x_codes[z][:, cols].bitcast(FP8X4),
-                rhs_scale=x_scale[4 * z :, cols],
+                rhs=x_codes[z][:, h, :, :].rearrange("p s v -> p (s v)").bitcast(FP8X4),
+                rhs_scale=x_scale[4 * z :, h, :, :].rearrange("p s v -> p (s v)"),
                 start=(z == 0),
                 stop=(z == PASSES - 1),
             )
 
-        cast_w1(*W1_CASTS[0])
-        nc.vector.tensor_copy(x_codes[0][:], x_table[0][:].indirect(offsets[:]))
-        nc.vector.tensor_copy(x_scale[:], x_scale_table[:].indirect(offsets[:]))
-        cast_w1(*W1_CASTS[1])
-        cast_w1(*W1_CASTS[2])
+        rounded_0 = keep.tile([P, PACK, P, PACK], BF16, name="rounded_0", tag="reused", align_bytes=64)
+        gather_pieces(x_scale, x_scale_table)
+        nc.vector.tensor_copy(x_codes[0][:].rearrange("p h s v -> p s h v"), x_table[0][:].indirect(offsets[:]))
+        cast_w1(rounded_0, 0, *W1_CASTS[0])
+        cast_w1(rounded_0, 0, *W1_CASTS[1])
         for t in range(PACK):
             if t % 2 == 0:
-                quantize_w1(0, t, t + 2, 0, P)
-            layer1(0, t, 1)
+                quantize_w1(rounded_0, 0, t, t + 2, 0, P)
             layer1(0, t, 0)
-        nc.vector.tensor_copy(x_codes[1][:], x_table[1][:].indirect(offsets[:]))
-        cast_w1(*W1_CASTS[3])
-        cast_w1(*W1_CASTS[4])
-        for t in range(PACK):
-            quantize_w1(1, t, t + 1, 0, HALF_M)
-        for cast in W1_CASTS[5:]:
-            cast_w1(*cast)
+            layer1(0, t, 1)
+        x_codes[1] = keep.tile([P, 2, 2, HALF_V], U32, name="x_codes1", tag="reused", align_bytes=64)
+        nc.vector.tensor_copy(x_codes[1][:].rearrange("p h s v -> p s h v"), x_table[1][:].indirect(offsets[:]))
+        rounded_1 = keep.tile([P, PACK, P, PACK], BF16, name="rounded_1", tag="w1_raw0", align_bytes=64)
+        for cast in W1_CASTS[2:]:
+            cast_w1(rounded_1, 0, *cast)
 
-        second = keep.tile([P, PACK, V], F32, name="second")
-        diff = keep.tile([P, PACK, V], F32, name="diff")
-        for t in range(PACK):
-            quantize_w1(1, t, t + 1, HALF_M, P)
-            layer1(1, t, 1)
-            layer1(1, t, 0)
-        for t in range(PACK):
-            nc.scalar.activation(out=second[:, t, :], in_=acc[t][1][:], func=ACT.Relu)
-            for cols in ([slice(0, V)] if t < PACK - 1 else [slice(0, HALF_V), slice(HALF_V, V)]):
-                nc.vector.scalar_tensor_tensor(
-                    out=diff[:, t, cols], in0=acc[t][0][:, cols], scalar=0.0, in1=second[:, t, cols], op0=ALU.max, op1=ALU.subtract
-                )
-
+        second = [keep.tile([P, PACK, HALF_V], F32, name=f"second{h}") for h in range(2)]
+        diff = [keep.tile([P, PACK, HALF_V], F32, name=f"diff{h}") for h in range(2)]
         z_bf = [keep.tile([P, HALF_V, PACK], BF16, name=f"z_bf{h}", align_bytes=64) for h in range(2)]
         z_codes = [keep.tile([P, HALF_V], U32, name=f"z_codes{h}", align_bytes=64) for h in range(2)]
         z_scale = [keep.tile([P, HALF_V], U8, name=f"z_scale{h}", align_bytes=64) for h in range(2)]
-        nc.scalar.activation(
-            out=z_bf[1][:].rearrange("p (c i) t -> p c t i", i=4),
-            in_=diff[:, :, HALF_V:].rearrange("p t (c i) -> p c t i", i=4),
-            func=ACT.Abs,
-        )
-        first_half = diff[:, :, :HALF_V].rearrange("p t v -> p v t")
-        nc.vector.scalar_tensor_tensor(out=z_bf[0][:], in0=first_half, scalar=-1.0, in1=first_half, op0=ALU.mult, op1=ALU.max)
 
+        for t in range(PACK):
+            quantize_w1(rounded_1, 1, t, t + 1, 0, P)
+            layer1(1, t, 0)
+        for t in range(PACK):
+            layer1(1, t, 1)
         for h in range(2):
+            for t in range(PACK):
+                nc.scalar.activation(out=second[h][:, t, :], in_=acc[h][t][:, 1, :], func=ACT.Relu)
+                nc.vector.scalar_tensor_tensor(
+                    out=diff[h][:, t, :], in0=acc[h][t][:, 0, :], scalar=0.0, in1=second[h][:, t, :], op0=ALU.max, op1=ALU.subtract
+                )
+
+        def abs_on_scalar(h, v0, v1):
+            nc.scalar.activation(
+                out=z_bf[h][:, v0:v1, :].rearrange("p (c i) t -> p c t i", i=4),
+                in_=diff[h][:, :, v0:v1].rearrange("p t (c i) -> p c t i", i=4),
+                func=ACT.Abs,
+            )
+
+        def abs_on_vector(h, v0, v1):
+            part = diff[h][:, :, v0:v1].rearrange("p t v -> p v t")
+            nc.vector.scalar_tensor_tensor(out=z_bf[h][:, v0:v1, :], in0=part, scalar=-1.0, in1=part, op0=ALU.mult, op1=ALU.max)
+
+        def layer2(h):
             nc.vector.quantize_mx(
                 out=z_codes[h][:].bitcast(FP8X4), scales=z_scale[h][:], in_=z_bf[h][:].rearrange("p v t -> p (v t)")
             )
-        for h in range(2):
-            res = psum.tile([N, V], F32, name=f"res{h}", tag=f"bank{h}_1")
+            res = psum.tile([N, 2, HALF_V], F32, name=f"res{h}", tag=f"bank0_{h}")
             nc.tensor.matmul_mx(
-                out=res[:, :HALF_V],
+                out=res[:, 0, :],
                 lhsT=w2_codes[:].bitcast(FP4X4),
                 lhsT_scale=w2_scale[:],
                 rhs=z_codes[h][:].bitcast(FP8X4),
@@ -167,8 +172,13 @@ def tile_picked_siam_abs_p_kernel(tc, x_words, x_scales, w1, w2_words, w2_scales
             staged = keep.tile([N, HALF_V], F32, name=f"staged{h}")
             cols = slice(h * HALF_V, (h + 1) * HALF_V)
             if h == 0:
-                nc.scalar.copy(out=staged[:], in_=res[:, :HALF_V])
-                nc.scalar.dma_start(out=out[:, cols], in_=staged[:])
+                nc.scalar.copy(out=staged[:], in_=res[:, 0, :])
             else:
-                nc.vector.tensor_copy(out=staged[:], in_=res[:, :HALF_V])
-                nc.sync.dma_start(out=out[:, cols], in_=staged[:])
+                nc.vector.tensor_copy(out=staged[:], in_=res[:, 0, :])
+            nc.sync.dma_start(out=out[:, cols], in_=staged[:])
+
+        abs_on_scalar(0, 0, HALF_V)
+        abs_on_vector(1, 0, 64)
+        abs_on_scalar(1, 64, HALF_V)
+        layer2(0)
+        layer2(1)

@@ -23,8 +23,7 @@ PASSES = K // K_PASS
 HALF_M = P // 2
 HALF_V = V // 2
 
-W1_LOADS = [(0, 0, 128), (1, 0, 64), (1, 64, 128)]
-W1_CASTS = [(0, 0, 84, "v"), (0, 84, 128, "s"), (1, 0, 16, "v"), (1, 16, 64, "s"), (2, 64, 106, "v"), (2, 106, 128, "s")]
+SCALAR_M = 80
 
 
 def tile_picked_siam_abs_p_kernel(tc, x_words, x_scales, w1, w2_words, w2_scales, offs, out):
@@ -38,16 +37,14 @@ def tile_picked_siam_abs_p_kernel(tc, x_words, x_scales, w1, w2_words, w2_scales
         w2_scale = keep.tile([P, N], U8, name="w2_scale", align_bytes=64)
         w2_codes = keep.tile([P, 2 * N], U8, name="w2_codes", align_bytes=64)
         x_table = [keep.tile([P, T], U32, name=f"x_table{z}", align_bytes=64) for z in range(PASSES)]
-        w1_raw = {}
+        w1_raw = [keep.tile([P, PACK, H], F32, name=f"w1_raw{z}", tag=f"w1_raw{z}", align_bytes=64) for z in range(PASSES)]
 
         nc.vector.memset(x_scale_table[:].bitcast(I32), 0)
         nc.vector.memset(w2_scale[:].bitcast(I32), 0)
 
-        def load_w1(c):
-            z, m0, m1 = W1_LOADS[c]
-            w1_raw[c] = keep.tile([P, PACK, PACK * (m1 - m0)], F32, name=f"w1_raw{c}", tag=f"w1_raw{c}", align_bytes=64)
-            rows = w1[z * K_PASS : (z + 1) * K_PASS, PACK * m0 : PACK * m1]
-            nc.sync.dma_start(out=w1_raw[c][:], in_=rows.rearrange("(p j) c -> p j c", j=PACK))
+        def load_w1(z):
+            rows = w1[z * K_PASS : (z + 1) * K_PASS, :]
+            nc.sync.dma_start(out=w1_raw[z][:], in_=rows.rearrange("(p j) c -> p j c", j=PACK))
 
         def load_x(z):
             nc.sync.dma_start(out=x_table[z][:].bitcast(I32), in_=x_words[z].rearrange("p c r -> p (c r)").bitcast(I32))
@@ -62,7 +59,6 @@ def tile_picked_siam_abs_p_kernel(tc, x_words, x_scales, w1, w2_words, w2_scales
         load_w1(0)
         load_x(1)
         load_w1(1)
-        load_w1(2)
         nc.sync.dma_start(out=w2_codes[:].bitcast(I32), in_=w2_words[0].bitcast(I32))
         for q in range(4):
             nc.sync.dma_start(
@@ -73,21 +69,25 @@ def tile_picked_siam_abs_p_kernel(tc, x_words, x_scales, w1, w2_words, w2_scales
         w1_codes = [keep.tile([P, PACK, P], U32, name=f"w1_codes{z}", align_bytes=64) for z in range(PASSES)]
         w1_scale = [keep.tile([P, PACK, P], U8, name=f"w1_scale{z}", align_bytes=64) for z in range(PASSES)]
 
-        def cast_w1(rounded, rounded_first, c, m0, m1, engine):
-            z, first, last = W1_LOADS[c]
-            dst = rounded[:, :, m0 - rounded_first : m1 - rounded_first, :].rearrange("p t m j -> p m j t")
-            src = w1_raw[c][:, :, PACK * (m0 - first) : PACK * (m1 - first)].rearrange("p j (m t) -> p m j t", t=PACK)
-            if engine == "v":
-                nc.vector.tensor_copy(out=dst, in_=src)
-            else:
-                nc.scalar.activation(out=dst, in_=src, func=ACT.Copy)
+        def round_w1(z, low, high):
+            def views(rounded, t0, m0, m1):
+                dst = rounded[:, :, m0:m1, :].rearrange("p t m j -> p m j t")
+                src = w1_raw[z][:].rearrange("p j (m t) -> p m j t", t=PACK)[:, m0:m1, :, t0 : t0 + 2]
+                return dst, src
 
-        def quantize_w1(rounded, z, t0, t1, m0, m1):
+            nc.vector.tensor_copy(*views(low, 0, 0, P))
+            nc.scalar.activation(*views(high, 2, 0, SCALAR_M), func=ACT.Copy)
+            nc.vector.tensor_copy(*views(high, 2, SCALAR_M, P))
+
+        def quantize_w1(z, rounded, t0):
             nc.vector.quantize_mx(
-                out=w1_codes[z][:, t0:t1, m0:m1].rearrange("p t m -> p (t m)").bitcast(FP8X4),
-                scales=w1_scale[z][:, t0:t1, m0:m1].rearrange("p t m -> p (t m)"),
-                in_=rounded[:, t0:t1, :, :].rearrange("p t m j -> p (t m j)"),
+                out=w1_codes[z][:, t0 : t0 + 2, :].rearrange("p t m -> p (t m)").bitcast(FP8X4),
+                scales=w1_scale[z][:, t0 : t0 + 2, :].rearrange("p t m -> p (t m)"),
+                in_=rounded[:].rearrange("p t m j -> p (t m j)"),
             )
+
+        def rounded_tile(name, tag):
+            return keep.tile([P, 2, P, PACK], BF16, name=name, tag=tag, align_bytes=64)
 
         x_scale = keep.tile([P, 2, 2, HALF_V], U8, name="x_scale", align_bytes=64)
         x_codes = {0: keep.tile([P, 2, 2, HALF_V], U32, name="x_codes0", align_bytes=64)}
@@ -110,21 +110,23 @@ def tile_picked_siam_abs_p_kernel(tc, x_words, x_scales, w1, w2_words, w2_scales
                 stop=(z == PASSES - 1),
             )
 
-        rounded_0 = keep.tile([P, PACK, P, PACK], BF16, name="rounded_0", tag="reused", align_bytes=64)
+        low_0 = rounded_tile("low_0", "reused_low")
+        high_0 = rounded_tile("high_0", "reused_high")
         gather_pieces(x_scale, x_scale_table)
         nc.vector.tensor_copy(x_codes[0][:].rearrange("p h s v -> p s h v"), x_table[0][:].indirect(offsets[:]))
-        cast_w1(rounded_0, 0, *W1_CASTS[0])
-        cast_w1(rounded_0, 0, *W1_CASTS[1])
+        round_w1(0, low_0, high_0)
+        quantize_w1(0, low_0, 0)
+        quantize_w1(0, high_0, 2)
         for t in range(PACK):
-            if t % 2 == 0:
-                quantize_w1(rounded_0, 0, t, t + 2, 0, P)
             layer1(0, t, 0)
             layer1(0, t, 1)
-        x_codes[1] = keep.tile([P, 2, 2, HALF_V], U32, name="x_codes1", tag="reused", align_bytes=64)
+        x_codes[1] = keep.tile([P, 2, 2, HALF_V], U32, name="x_codes1", tag="reused_high", align_bytes=64)
         nc.vector.tensor_copy(x_codes[1][:].rearrange("p h s v -> p s h v"), x_table[1][:].indirect(offsets[:]))
-        rounded_1 = keep.tile([P, PACK, P, PACK], BF16, name="rounded_1", tag="w1_raw0", align_bytes=64)
-        for cast in W1_CASTS[2:]:
-            cast_w1(rounded_1, 0, *cast)
+        low_1 = rounded_tile("low_1", "w1_raw0")
+        high_1 = rounded_tile("high_1", "reused_low")
+        round_w1(1, low_1, high_1)
+        quantize_w1(1, low_1, 0)
+        quantize_w1(1, high_1, 2)
 
         second = [keep.tile([P, PACK, HALF_V], F32, name=f"second{h}") for h in range(2)]
         diff = [keep.tile([P, PACK, HALF_V], F32, name=f"diff{h}") for h in range(2)]
@@ -132,11 +134,9 @@ def tile_picked_siam_abs_p_kernel(tc, x_words, x_scales, w1, w2_words, w2_scales
         z_codes = [keep.tile([P, HALF_V], U32, name=f"z_codes{h}", align_bytes=64) for h in range(2)]
         z_scale = [keep.tile([P, HALF_V], U8, name=f"z_scale{h}", align_bytes=64) for h in range(2)]
 
-        for t in range(PACK):
-            quantize_w1(rounded_1, 1, t, t + 1, 0, P)
-            layer1(1, t, 0)
-        for t in range(PACK):
-            layer1(1, t, 1)
+        for h in range(2):
+            for t in range(PACK):
+                layer1(1, t, h)
         for h in range(2):
             for t in range(PACK):
                 nc.scalar.activation(out=second[h][:, t, :], in_=acc[h][t][:, 1, :], func=ACT.Relu)

@@ -39,7 +39,7 @@ def tile_picked_siam_abs_p_kernel(tc, x_words, x_scales, w1, w2_words, w2_scales
         x_table = [keep.tile([P, T], U32, name=f"x_table{z}", align_bytes=64) for z in range(PASSES)]
         w1_raw = [keep.tile([P, PACK, H], F32, name=f"w1_raw{z}", tag=f"w1_raw{z}", align_bytes=64) for z in range(PASSES)]
 
-        nc.vector.memset(x_scale_table[:].bitcast(I32), 0)
+        nc.gpsimd.memset(x_scale_table[:].bitcast(I32), 0)
         nc.vector.memset(w2_scale[:].bitcast(I32), 0)
 
         def load_w1(z):
@@ -49,17 +49,17 @@ def tile_picked_siam_abs_p_kernel(tc, x_words, x_scales, w1, w2_words, w2_scales
         def load_x(z):
             nc.sync.dma_start(out=x_table[z][:].bitcast(I32), in_=x_words[z].rearrange("p c r -> p (c r)").bitcast(I32))
 
+        load_x(0)
+        nc.sync.dma_start(offsets[:], offs)
+        nc.sync.dma_start(out=w2_codes[:].bitcast(I32), in_=w2_words[0].bitcast(I32))
         for q in range(4):
-            nc.scalar.dma_start(
+            nc.sync.dma_start(
                 out=x_scale_table[32 * q : 32 * q + 4 * PASSES, :].bitcast(I32),
                 in_=x_scales[:, 4 * q : 4 * q + 4, :].bitcast(I32),
             )
-        nc.sync.dma_start(offsets[:], offs)
-        load_x(0)
         load_w1(0)
         load_x(1)
         load_w1(1)
-        nc.sync.dma_start(out=w2_codes[:].bitcast(I32), in_=w2_words[0].bitcast(I32))
         for q in range(4):
             nc.sync.dma_start(
                 out=w2_scale[32 * q : 32 * q + 4, :].bitcast(I32),
@@ -112,8 +112,8 @@ def tile_picked_siam_abs_p_kernel(tc, x_words, x_scales, w1, w2_words, w2_scales
 
         low_0 = rounded_tile("low_0", "reused_low")
         high_0 = rounded_tile("high_0", "reused_high")
-        gather_pieces(x_scale, x_scale_table)
         nc.vector.tensor_copy(x_codes[0][:].rearrange("p h s v -> p s h v"), x_table[0][:].indirect(offsets[:]))
+        gather_pieces(x_scale, x_scale_table)
         round_w1(0, low_0, high_0)
         quantize_w1(0, low_0, 0)
         quantize_w1(0, high_0, 2)

from contextlib import ExitStack

import concourse.mybir as mybir

K, T, S, V, H, N = 1024, 1024, 512, 256, 512, 128
FLOPS = 2 * K * H * S + 2 * H * N * V

F32 = mybir.dt.float32
BF16 = mybir.dt.bfloat16
I32 = mybir.dt.int32
U32 = mybir.dt.uint32
U16 = mybir.dt.uint16
U8 = mybir.dt.uint8
FP8X4 = mybir.dt.float8_e4m3fn_x4
FP4X4 = mybir.dt.float4_e2m1fn_x4
ACT = mybir.ActivationFunctionType
ALU = mybir.AluOpType

P = 128
PACK = 4
K_PASS = P * PACK
PASSES = K // K_PASS
HALF_M = P // 2
HALF_V = V // 2

SCALAR_M = 80


def tile_picked_siam_abs_p_kernel(tc, x_words, x_scales, w1, w2_words, w2_scales, offs, out):
    nc = tc.nc
    with ExitStack() as ctx:
        keep = ctx.enter_context(tc.tile_pool(name="keep", bufs=1))
        psum = ctx.enter_context(tc.psum_pool(name="psum", bufs=1))

        offsets = keep.tile([P, S // 16], U16, name="offsets")
        x_scale_table = keep.tile([P, T], U8, name="x_scale_table", align_bytes=64)
        w2_scale = keep.tile([P, N], U8, name="w2_scale", align_bytes=64)
        w2_codes = keep.tile([P, 2 * N], U8, name="w2_codes", align_bytes=64)
        x_table = [keep.tile([P, T], U32, name=f"x_table{z}", align_bytes=64) for z in range(PASSES)]
        w1_raw = [keep.tile([P, PACK, H], F32, name=f"w1_raw{z}", tag=f"w1_raw{z}", align_bytes=64) for z in range(PASSES)]

        nc.gpsimd.memset(x_scale_table[:].bitcast(I32), 0)
        nc.vector.memset(w2_scale[:].bitcast(I32), 0)

        def load_w1(z):
            rows = w1[z * K_PASS : (z + 1) * K_PASS, :]
            nc.sync.dma_start(out=w1_raw[z][:], in_=rows.rearrange("(p j) c -> p j c", j=PACK))

        def load_x(z):
            nc.sync.dma_start(out=x_table[z][:].bitcast(I32), in_=x_words[z].rearrange("p c r -> p (c r)").bitcast(I32))

        load_x(0)
        nc.sync.dma_start(offsets[:], offs)
        nc.sync.dma_start(out=w2_codes[:].bitcast(I32), in_=w2_words[0].bitcast(I32))
        for q in range(4):
            nc.sync.dma_start(
                out=x_scale_table[32 * q : 32 * q + 4 * PASSES, :].bitcast(I32),
                in_=x_scales[:, 4 * q : 4 * q + 4, :].bitcast(I32),
            )
        load_w1(0)
        load_x(1)
        load_w1(1)
        for q in range(4):
            nc.sync.dma_start(
                out=w2_scale[32 * q : 32 * q + 4, :].bitcast(I32),
                in_=w2_scales[0, 4 * q : 4 * q + 4, :].bitcast(I32),
            )

        w1_codes = [keep.tile([P, PACK, P], U32, name=f"w1_codes{z}", align_bytes=64) for z in range(PASSES)]
        w1_scale = [keep.tile([P, PACK, P], U8, name=f"w1_scale{z}", align_bytes=64) for z in range(PASSES)]

        def round_w1(z, low, high):
            def views(rounded, t0, m0, m1):
                dst = rounded[:, :, m0:m1, :].rearrange("p t m j -> p m j t")
                src = w1_raw[z][:].rearrange("p j (m t) -> p m j t", t=PACK)[:, m0:m1, :, t0 : t0 + 2]
                return dst, src

            nc.vector.tensor_copy(*views(low, 0, 0, P))
            nc.scalar.activation(*views(high, 2, 0, SCALAR_M), func=ACT.Copy)
            nc.vector.tensor_copy(*views(high, 2, SCALAR_M, P))

        def quantize_w1(z, rounded, t0):
            nc.vector.quantize_mx(
                out=w1_codes[z][:, t0 : t0 + 2, :].rearrange("p t m -> p (t m)").bitcast(FP8X4),
                scales=w1_scale[z][:, t0 : t0 + 2, :].rearrange("p t m -> p (t m)"),
                in_=rounded[:].rearrange("p t m j -> p (t m j)"),
            )

        def rounded_tile(name, tag):
            return keep.tile([P, 2, P, PACK], BF16, name=name, tag=tag, align_bytes=64)

        x_scale = keep.tile([P, 2, 2, HALF_V], U8, name="x_scale", align_bytes=64)
        x_codes = {0: keep.tile([P, 2, 2, HALF_V], U32, name="x_codes0", align_bytes=64)}
        acc = [[psum.tile([P, 2, HALF_V], F32, name=f"acc{h}_{t}", tag=f"bank{h}_{t}") for t in range(PACK)] for h in range(2)]

        def gather_pieces(picked, table):
            for h in range(2):
                for side in range(2):
                    first = (side * V + h * HALF_V) // 16
                    nc.vector.tensor_copy(picked[:, h, side, :], table[:].indirect(offsets[:, first : first + HALF_V // 16]))

        def layer1(z, t, h):
            nc.tensor.matmul_mx(
                out=acc[h][t][:].rearrange("p s v -> p (s v)"),
                lhsT=w1_codes[z][:, t, :].bitcast(FP8X4),
                lhsT_scale=w1_scale[z][:, t, :],
                rhs=x_codes[z][:, h, :, :].rearrange("p s v -> p (s v)").bitcast(FP8X4),
                rhs_scale=x_scale[4 * z :, h, :, :].rearrange("p s v -> p (s v)"),
                start=(z == 0),
                stop=(z == PASSES - 1),
            )

        low_0 = rounded_tile("low_0", "reused_low")
        high_0 = rounded_tile("high_0", "reused_high")
        nc.vector.tensor_copy(x_codes[0][:].rearrange("p h s v -> p s h v"), x_table[0][:].indirect(offsets[:]))
        gather_pieces(x_scale, x_scale_table)
        round_w1(0, low_0, high_0)
        quantize_w1(0, low_0, 0)
        quantize_w1(0, high_0, 2)
        for t in range(PACK):
            layer1(0, t, 0)
            layer1(0, t, 1)
        x_codes[1] = keep.tile([P, 2, 2, HALF_V], U32, name="x_codes1", tag="reused_high", align_bytes=64)
        nc.vector.tensor_copy(x_codes[1][:].rearrange("p h s v -> p s h v"), x_table[1][:].indirect(offsets[:]))
        low_1 = rounded_tile("low_1", "w1_raw0")
        high_1 = rounded_tile("high_1", "reused_low")
        round_w1(1, low_1, high_1)
        quantize_w1(1, low_1, 0)
        quantize_w1(1, high_1, 2)

        second = [keep.tile([P, PACK, HALF_V], F32, name=f"second{h}") for h in range(2)]
        diff = [keep.tile([P, PACK, HALF_V], F32, name=f"diff{h}") for h in range(2)]
        z_bf = [keep.tile([P, HALF_V, PACK], BF16, name=f"z_bf{h}", align_bytes=64) for h in range(2)]
        z_codes = [keep.tile([P, HALF_V], U32, name=f"z_codes{h}", align_bytes=64) for h in range(2)]
        z_scale = [keep.tile([P, HALF_V], U8, name=f"z_scale{h}", align_bytes=64) for h in range(2)]

        for h in range(2):
            for t in range(PACK):
                layer1(1, t, h)
        for h in range(2):
            for t in range(PACK):
                nc.scalar.activation(out=second[h][:, t, :], in_=acc[h][t][:, 1, :], func=ACT.Relu)
                nc.vector.scalar_tensor_tensor(
                    out=diff[h][:, t, :], in0=acc[h][t][:, 0, :], scalar=0.0, in1=second[h][:, t, :], op0=ALU.max, op1=ALU.subtract
                )

        def abs_on_scalar(h, v0, v1):
            nc.scalar.activation(
                out=z_bf[h][:, v0:v1, :].rearrange("p (c i) t -> p c t i", i=4),
                in_=diff[h][:, :, v0:v1].rearrange("p t (c i) -> p c t i", i=4),
                func=ACT.Abs,
            )

        def abs_on_vector(h, v0, v1):
            part = diff[h][:, :, v0:v1].rearrange("p t v -> p v t")
            nc.vector.scalar_tensor_tensor(out=z_bf[h][:, v0:v1, :], in0=part, scalar=-1.0, in1=part, op0=ALU.mult, op1=ALU.max)

        def layer2(h):
            nc.vector.quantize_mx(
                out=z_codes[h][:].bitcast(FP8X4), scales=z_scale[h][:], in_=z_bf[h][:].rearrange("p v t -> p (v t)")
            )
            res = psum.tile([N, 2, HALF_V], F32, name=f"res{h}", tag=f"bank0_{h}")
            nc.tensor.matmul_mx(
                out=res[:, 0, :],
                lhsT=w2_codes[:].bitcast(FP4X4),
                lhsT_scale=w2_scale[:],
                rhs=z_codes[h][:].bitcast(FP8X4),
                rhs_scale=z_scale[h][:],
                start=True,
                stop=True,
            )
            staged = keep.tile([N, HALF_V], F32, name=f"staged{h}")
            cols = slice(h * HALF_V, (h + 1) * HALF_V)
            if h == 0:
                nc.scalar.copy(out=staged[:], in_=res[:, 0, :])
            else:
                nc.vector.tensor_copy(out=staged[:], in_=res[:, 0, :])
            nc.sync.dma_start(out=out[:, cols], in_=staged[:])

        abs_on_scalar(0, 0, HALF_V)
        abs_on_vector(1, 0, 64)
        abs_on_scalar(1, 64, HALF_V)
        layer2(0)
        layer2(1)
